import numpy as np
import ml_dtypes


def mxq(x, axis, fmt="e4m3"):
    dtype, down = {"e4m3": (ml_dtypes.float8_e4m3fn, 7), "e5m2": (ml_dtypes.float8_e5m2, 14)}[fmt]
    v = np.moveaxis(np.asarray(x, np.float32).astype(ml_dtypes.bfloat16).astype(np.float64), axis, -1)
    blocks = v.reshape(v.shape[:-1] + (-1, 32))
    amax = np.abs(blocks).max(-1, keepdims=True)
    byte = np.maximum(np.where(amax > 0, np.frexp(amax)[1] - 1 + 127, 0) - down, 1)
    scale = np.exp2(byte - 127.0)
    codes = (blocks / scale).astype(np.float32).astype(dtype).astype(np.float64)
    return np.moveaxis((codes * scale).reshape(v.shape), -1, axis)


WIDE = False


def mx_kscale(k):
    if not WIDE:
        return np.ones(k)
    levels = np.array([10, -10, 5, -5, 0])
    if k % 512:
        return np.exp2(np.random.permutation(np.resize(levels, k // 32))).repeat(32)
    a = np.empty((k // 512, 16))
    for p in range(k // 512):
        a[p, :8] = np.random.permutation(np.resize(levels, 8))
        for g in range(8):
            far = levels[np.abs(levels - a[p, g]) >= 10]
            a[p, g + 8] = far[np.random.randint(len(far))]
    return np.exp2(a.ravel()).repeat(32)


def f64(x):
    return np.asarray(x).astype(np.float64)


def striped(idx):
    return np.tile(idx.reshape(-1, 16).T, (8, 1)).astype(np.uint16)


def unstriped(offs):
    return offs[:16].T.reshape(-1).astype(np.int64)


def pack_weight(w):
    k, n = w.shape
    w = f64(np.asarray(w, np.float32).astype(ml_dtypes.bfloat16)).reshape(k // 32, 32, n)
    amax = np.abs(w).max(1)
    byte = np.clip(np.where(amax > 0, np.frexp(amax)[1] - 1 + 127 - 7, 1), 1, 254)
    scaled = (w * np.exp2(127.0 - byte)[:, None, :]).reshape(k, n).astype(np.float32)
    words = np.ascontiguousarray(scaled.reshape(k // 512, 128, 4, n).transpose(0, 1, 3, 2)).astype(ml_dtypes.float8_e4m3fn).view(np.uint8)
    return words, np.ascontiguousarray(byte.astype(np.uint8).reshape(k // 512, 16, n))


def unpack_weight(words, scales):
    g, p, n, _ = words.shape
    vals = np.ascontiguousarray(words).view(ml_dtypes.float8_e4m3fn).astype(np.float64) * np.repeat(np.exp2(scales.astype(np.float64) - 127.0), 8, axis=1)[..., None]
    return vals.transpose(0, 1, 3, 2).reshape(g * 512, n)


K, T, S, N, R = 512, 2048, 512, 256, 256


def setup_inputs():
    n = np.random.standard_normal
    s = mx_kscale(K)[:, None]
    c = mx_kscale(S)
    packed_xT = pack_weight(n((K, T)) * s)
    return {
        "x_words": packed_xT[0],
        "x_scales": packed_xT[1],
        "cT": (n((K, N)) / np.sqrt(K) / s).astype(np.float32),
        "area": (np.random.uniform(0.5, 1.0, (S, 1)) * c[:, None]).astype(np.float32),
        "qm": (n((S, R)) / np.sqrt(S) / c[:, None]).astype(np.float32),
        "cur": (n((R, N))).astype(np.float32),
        "offs": striped(np.random.permutation(T)[:S]),
        "right": striped(np.random.permutation(T)[:S]),
    }


def reference(x_words, x_scales, cT, area, qm, cur, offs, right):
    xq = unpack_weight(x_words, x_scales)[:, unstriped(offs)]
    cTq = mxq(f64(cT), 0, "e4m3")
    lt = xq.T @ cTq
    x_right = unpack_weight(x_words, x_scales)[:, unstriped(right)]
    rt = x_right.T @ cTq
    jump = rt - lt
    flux = 0.5 * (lt + rt) - (0.5 * np.abs(jump))
    fa = f64(area) * flux
    return f64(cur) - (0.5 * ((mxq(f64(qm), 0, "e4m3").T @ mxq(fa, 0, "e4m3"))))

@@ -1,0 +1,125 @@
+from contextlib import ExitStack
+
+import concourse.mybir as mybir
+
+K, T, S, N, R = 512, 2048, 512, 256, 256
+FLOPS = 2 * (2 * S * K * N + S * R * N)
+
+F32 = mybir.dt.float32
+BF16 = mybir.dt.bfloat16
+I32 = mybir.dt.int32
+U32 = mybir.dt.uint32
+U16 = mybir.dt.uint16
+U8 = mybir.dt.uint8
+FP8X4 = mybir.dt.float8_e4m3fn_x4
+ALU = mybir.AluOpType
+
+P = 128
+PACK = 4
+HALF = 128
+
+
+def tile_picked_yrus_upw_p_kernel(tc, x_words, x_scales, cT, area, qm, cur, offs, right, out):
+    nc = tc.nc
+    with ExitStack() as ctx:
+        lists = ctx.enter_context(tc.tile_pool(name="lists", bufs=1))
+        sb = ctx.enter_context(tc.tile_pool(name="sb", bufs=1))
+        ps = ctx.enter_context(tc.psum_pool(name="ps", bufs=1))
+
+        left_list = lists.tile([P, S // 16], U16, name="left_list")
+        right_list = lists.tile([P, S // 16], U16, name="right_list")
+        scale_table = sb.tile([P, T], U8, name="scale_table", align_bytes=64)
+        word_table = sb.tile([P, T], U32, name="word_table", align_bytes=64)
+        c_raw = sb.tile([P, PACK, N], F32, name="c_raw")
+        q_raw = sb.tile([P, PACK, R], F32, name="q_raw")
+        area_sb = sb.tile([P, PACK], F32, name="area_sb")
+        cur_sb = sb.tile([P, R // P, N], F32, name="cur_sb")
+
+        nc.vector.memset(scale_table[:].bitcast(I32), 0)
+        nc.sync.dma_start(left_list[:], offs)
+        for q in range(4):
+            nc.sync.dma_start(scale_table[32 * q : 32 * q + 4, :].bitcast(I32), x_scales[0, 4 * q : 4 * q + 4, :].bitcast(I32))
+        nc.sync.dma_start(right_list[:], right)
+        nc.sync.dma_start(c_raw[:], cT.rearrange("(p j) m -> p j m", j=PACK))
+        nc.sync.dma_start(word_table[:].bitcast(I32), x_words[0].rearrange("p c b -> p (c b)").bitcast(I32))
+        nc.sync.dma_start(q_raw[:], qm.rearrange("(p j) r -> p j r", j=PACK))
+        nc.sync.dma_start(area_sb[:], area.rearrange("(p j) o -> p (j o)", j=PACK))
+        nc.sync.dma_start(cur_sb[:], cur.rearrange("(e p) m -> p e m", p=P))
+
+        picked_scales = sb.tile([P, 2, S], U8, name="picked_scales", align_bytes=64)
+        dealt_scales = sb.tile([P, 2, S], U8, name="dealt_scales", align_bytes=64)
+        both_lists = (left_list, right_list)
+        for side in range(2):
+            nc.vector.tensor_copy(picked_scales[:, side, :], scale_table[:].indirect(both_lists[side][:]))
+        nc.vector.tensor_copy(
+            dealt_scales[:].rearrange("q s (j p) -> q s j p", j=PACK),
+            picked_scales[:].rearrange("q s (p j) -> q s j p", j=PACK),
+        )
+
+        c_bf = sb.tile([P, N, PACK], BF16, name="c_bf", align_bytes=64)
+        c_codes = sb.tile([P, N], U32, name="c_codes", align_bytes=64)
+        c_scales = sb.tile([P, N], U8, name="c_scales", align_bytes=64)
+        nc.scalar.copy(c_bf[:], c_raw[:].rearrange("p j m -> p m j"))
+        nc.vector.quantize_mx(out=c_codes[:].bitcast(FP8X4), scales=c_scales[:], in_=c_bf[:].rearrange("p m j -> p (m j)"))
+
+        states = []
+        for side in range(2):
+            words = sb.tile([P, S], U32, name=f"words{side}", align_bytes=64)
+            nc.vector.tensor_copy(words[:].rearrange("q (j p) -> q p j", j=PACK), word_table[:].indirect(both_lists[side][:]))
+            banks = []
+            for h in range(N // HALF):
+                cols = slice(h * HALF, (h + 1) * HALF)
+                bank = ps.tile([P, PACK, HALF], F32, name=f"state{side}{h}")
+                for j in range(PACK):
+                    faces = slice(j * P, (j + 1) * P)
+                    nc.tensor.matmul_mx(
+                        out=bank[:, j, :],
+                        lhsT=words[:, faces].bitcast(FP8X4),
+                        lhsT_scale=dealt_scales[:, side, faces],
+                        rhs=c_codes[:, cols].bitcast(FP8X4),
+                        rhs_scale=c_scales[:, cols],
+                        start=True,
+                        stop=True,
+                    )
+                banks.append(bank)
+            states.append(banks)
+
+        q_bf = sb.tile([P, R, PACK], BF16, name="q_bf", align_bytes=64)
+        q_codes = sb.tile([P, R], U32, name="q_codes", align_bytes=64)
+        q_scales = sb.tile([P, R], U8, name="q_scales", align_bytes=64)
+
+        halves = range(N // HALF)
+        left_sb = [sb.tile([P, HALF, PACK], F32, name=f"left_sb{h}") for h in halves]
+        flux = [sb.tile([P, HALF, PACK], F32, name=f"flux{h}") for h in halves]
+        fa_bf = [sb.tile([P, HALF, PACK], BF16, name=f"fa_bf{h}", align_bytes=64) for h in halves]
+        fa_codes = [sb.tile([P, HALF], U32, name=f"fa_codes{h}", align_bytes=64) for h in halves]
+        fa_scales = [sb.tile([P, HALF], U8, name=f"fa_scales{h}", align_bytes=64) for h in halves]
+        result = [sb.tile([P, R // P, HALF], F32, name=f"result{h}") for h in halves]
+
+        nc.scalar.copy(q_bf[:], q_raw[:].rearrange("p j r -> p r j"))
+        for h in halves:
+            nc.scalar.copy(left_sb[h][:], states[0][h][:].rearrange("p j m -> p m j"))
+        nc.vector.quantize_mx(out=q_codes[:].bitcast(FP8X4), scales=q_scales[:], in_=q_bf[:].rearrange("p r j -> p (r j)"))
+        for h in halves:
+            nc.vector.tensor_tensor(flux[h][:], states[1][h][:].rearrange("p j m -> p m j"), left_sb[h][:], ALU.min)
+        for h in halves:
+            nc.vector.tensor_tensor(fa_bf[h][:], flux[h][:], area_sb[:].unsqueeze(1).to_broadcast([P, HALF, PACK]), ALU.mult)
+        for h in halves:
+            nc.vector.quantize_mx(out=fa_codes[h][:].bitcast(FP8X4), scales=fa_scales[h][:], in_=fa_bf[h][:].rearrange("p m j -> p (m j)"))
+        out_view = out.rearrange("(e p) m -> p e m", p=P)
+        for h in halves:
+            cols = slice(h * HALF, (h + 1) * HALF)
+            acc = ps.tile([P, R // P, HALF], F32, name=f"acc{h}")
+            for e in range(R // P):
+                rows = slice(e * P, (e + 1) * P)
+                nc.tensor.matmul_mx(
+                    out=acc[:, e, :],
+                    lhsT=q_codes[:, rows].bitcast(FP8X4),
+                    lhsT_scale=q_scales[:, rows],
+                    rhs=fa_codes[h][:].bitcast(FP8X4),
+                    rhs_scale=fa_scales[h][:],
+                    start=True,
+                    stop=True,
+                )
+            nc.vector.scalar_tensor_tensor(result[h][:], acc[:], -0.5, cur_sb[:, :, cols], ALU.mult, ALU.add)
+            (nc.sync, nc.scalar)[h].dma_start(out_view[:, :, cols], result[h][:])

@@ -17,6 +17,7 @@ ALU = mybir.AluOpType
 P = 128
 PACK = 4
 HALF = 128
+RUN = 4
 
 
 def tile_picked_yrus_upw_p_kernel(tc, x_words, x_scales, cT, area, qm, cur, offs, right, out):
@@ -31,7 +32,7 @@ def tile_picked_yrus_upw_p_kernel(tc, x_words, x_scales, cT, area, qm, cur, offs
         scale_table = sb.tile([P, T], U8, name="scale_table", align_bytes=64)
         word_table = sb.tile([P, T], U32, name="word_table", align_bytes=64)
         c_raw = sb.tile([P, PACK, N], F32, name="c_raw")
-        q_raw = sb.tile([P, PACK, R], F32, name="q_raw")
+        q_raw = sb.tile([P, PACK, R], F32, name="q_raw", tag="q_raw_then_left")
         area_sb = sb.tile([P, PACK], F32, name="area_sb")
         cur_sb = sb.tile([P, R // P, N], F32, name="cur_sb")
 
@@ -42,8 +43,13 @@ def tile_picked_yrus_upw_p_kernel(tc, x_words, x_scales, cT, area, qm, cur, offs
         nc.sync.dma_start(right_list[:], right)
         nc.sync.dma_start(c_raw[:], cT.rearrange("(p j) m -> p j m", j=PACK))
         nc.sync.dma_start(word_table[:].bitcast(I32), x_words[0].rearrange("p c b -> p (c b)").bitcast(I32))
-        nc.sync.dma_start(q_raw[:], qm.rearrange("(p j) r -> p j r", j=PACK))
-        nc.sync.dma_start(area_sb[:], area.rearrange("(p j) o -> p (j o)", j=PACK))
+        qm_dealt = qm.rearrange("(c j i) r -> i c j r", j=PACK, i=RUN)
+        area_dealt = area.rearrange("(c j i) o -> i c (j o)", j=PACK, i=RUN)
+        for i in range(RUN):
+            nc.sync.dma_start(q_raw[i:P:RUN, :, :], qm_dealt[i])
+        with nc.allow_non_contiguous_dma(reason="one area a face"):
+            for i in range(RUN):
+                nc.sync.dma_start(area_sb[i:P:RUN, :], area_dealt[i])
         nc.sync.dma_start(cur_sb[:], cur.rearrange("(e p) m -> p e m", p=P))
 
         picked_scales = sb.tile([P, 2, S], U8, name="picked_scales", align_bytes=64)
@@ -51,21 +57,21 @@ def tile_picked_yrus_upw_p_kernel(tc, x_words, x_scales, cT, area, qm, cur, offs
         both_lists = (left_list, right_list)
         for side in range(2):
             nc.vector.tensor_copy(picked_scales[:, side, :], scale_table[:].indirect(both_lists[side][:]))
-        nc.vector.tensor_copy(
-            dealt_scales[:].rearrange("q s (j p) -> q s j p", j=PACK),
-            picked_scales[:].rearrange("q s (p j) -> q s j p", j=PACK),
-        )
 
-        c_bf = sb.tile([P, N, PACK], BF16, name="c_bf", align_bytes=64)
+        c_bf = sb.tile([P, N, PACK], BF16, name="c_bf", tag="c_bf_then_words", align_bytes=64)
         c_codes = sb.tile([P, N], U32, name="c_codes", align_bytes=64)
         c_scales = sb.tile([P, N], U8, name="c_scales", align_bytes=64)
         nc.scalar.copy(c_bf[:], c_raw[:].rearrange("p j m -> p m j"))
         nc.vector.quantize_mx(out=c_codes[:].bitcast(FP8X4), scales=c_scales[:], in_=c_bf[:].rearrange("p m j -> p (m j)"))
 
+        words = sb.tile([P, 2, S], U32, name="words", tag="c_bf_then_words", align_bytes=64)
         states = []
         for side in range(2):
-            words = sb.tile([P, S], U32, name=f"words{side}", align_bytes=64)
-            nc.vector.tensor_copy(words[:].rearrange("q (j p) -> q p j", j=PACK), word_table[:].indirect(both_lists[side][:]))
+            nc.vector.tensor_copy(
+                dealt_scales[:, side, :].bitcast(I32).rearrange("q (j c) -> q j c", j=PACK),
+                picked_scales[:, side, :].bitcast(I32).rearrange("q (c j) -> q j c", j=PACK),
+            )
+            nc.vector.tensor_copy(words[:, side, :].rearrange("q (j c i) -> q c j i", j=PACK, i=RUN), word_table[:].indirect(both_lists[side][:]))
             banks = []
             for h in range(N // HALF):
                 cols = slice(h * HALF, (h + 1) * HALF)
@@ -74,7 +80,7 @@ def tile_picked_yrus_upw_p_kernel(tc, x_words, x_scales, cT, area, qm, cur, offs
                     faces = slice(j * P, (j + 1) * P)
                     nc.tensor.matmul_mx(
                         out=bank[:, j, :],
-                        lhsT=words[:, faces].bitcast(FP8X4),
+                        lhsT=words[:, side, faces].bitcast(FP8X4),
                         lhsT_scale=dealt_scales[:, side, faces],
                         rhs=c_codes[:, cols].bitcast(FP8X4),
                         rhs_scale=c_scales[:, cols],
@@ -84,31 +90,31 @@ def tile_picked_yrus_upw_p_kernel(tc, x_words, x_scales, cT, area, qm, cur, offs
                 banks.append(bank)
             states.append(banks)
 
-        q_bf = sb.tile([P, R, PACK], BF16, name="q_bf", align_bytes=64)
+        q_bf = sb.tile([P, R, PACK], BF16, name="q_bf", tag="q_bf_then_flux", align_bytes=64)
         q_codes = sb.tile([P, R], U32, name="q_codes", align_bytes=64)
         q_scales = sb.tile([P, R], U8, name="q_scales", align_bytes=64)
+        nc.scalar.copy(q_bf[:], q_raw[:].rearrange("p j r -> p r j"))
+        nc.vector.quantize_mx(out=q_codes[:].bitcast(FP8X4), scales=q_scales[:], in_=q_bf[:].rearrange("p r j -> p (r j)"))
 
         halves = range(N // HALF)
-        left_sb = [sb.tile([P, HALF, PACK], F32, name=f"left_sb{h}") for h in halves]
-        flux = [sb.tile([P, HALF, PACK], F32, name=f"flux{h}") for h in halves]
+        left_sb = sb.tile([P, N, PACK], F32, name="left_sb", tag="q_raw_then_left")
+        flux = sb.tile([P, N, PACK], F32, name="flux", tag="q_bf_then_flux", align_bytes=64)
         fa_bf = [sb.tile([P, HALF, PACK], BF16, name=f"fa_bf{h}", align_bytes=64) for h in halves]
         fa_codes = [sb.tile([P, HALF], U32, name=f"fa_codes{h}", align_bytes=64) for h in halves]
         fa_scales = [sb.tile([P, HALF], U8, name=f"fa_scales{h}", align_bytes=64) for h in halves]
         result = [sb.tile([P, R // P, HALF], F32, name=f"result{h}") for h in halves]
+        cols = [slice(h * HALF, (h + 1) * HALF) for h in halves]
 
-        nc.scalar.copy(q_bf[:], q_raw[:].rearrange("p j r -> p r j"))
         for h in halves:
-            nc.scalar.copy(left_sb[h][:], states[0][h][:].rearrange("p j m -> p m j"))
-        nc.vector.quantize_mx(out=q_codes[:].bitcast(FP8X4), scales=q_scales[:], in_=q_bf[:].rearrange("p r j -> p (r j)"))
+            nc.scalar.copy(left_sb[:, cols[h], :], states[0][h][:].rearrange("p j m -> p m j"))
         for h in halves:
-            nc.vector.tensor_tensor(flux[h][:], states[1][h][:].rearrange("p j m -> p m j"), left_sb[h][:], ALU.min)
+            nc.vector.tensor_tensor(flux[:, cols[h], :], states[1][h][:].rearrange("p j m -> p m j"), left_sb[:, cols[h], :], ALU.min)
         for h in halves:
-            nc.vector.tensor_tensor(fa_bf[h][:], flux[h][:], area_sb[:].unsqueeze(1).to_broadcast([P, HALF, PACK]), ALU.mult)
+            nc.vector.tensor_tensor(fa_bf[h][:], flux[:, cols[h], :], area_sb[:].unsqueeze(1).to_broadcast([P, HALF, PACK]), ALU.mult)
         for h in halves:
             nc.vector.quantize_mx(out=fa_codes[h][:].bitcast(FP8X4), scales=fa_scales[h][:], in_=fa_bf[h][:].rearrange("p m j -> p (m j)"))
         out_view = out.rearrange("(e p) m -> p e m", p=P)
         for h in halves:
-            cols = slice(h * HALF, (h + 1) * HALF)
             acc = ps.tile([P, R // P, HALF], F32, name=f"acc{h}")
             for e in range(R // P):
                 rows = slice(e * P, (e + 1) * P)
@@ -121,5 +127,5 @@ def tile_picked_yrus_upw_p_kernel(tc, x_words, x_scales, cT, area, qm, cur, offs
                     start=True,
                     stop=True,
                 )
-            nc.vector.scalar_tensor_tensor(result[h][:], acc[:], -0.5, cur_sb[:, :, cols], ALU.mult, ALU.add)
-            (nc.sync, nc.scalar)[h].dma_start(out_view[:, :, cols], result[h][:])
+            nc.vector.scalar_tensor_tensor(result[h][:], acc[:], -0.5, cur_sb[:, :, cols[h]], ALU.mult, ALU.add)
+            (nc.sync, nc.scalar)[h].dma_start(out_view[:, :, cols[h]], result[h][:])

@@ -38,8 +38,8 @@ def tile_picked_yrus_upw_p_kernel(tc, x_words, x_scales, cT, area, qm, cur, offs
 
         nc.vector.memset(scale_table[:].bitcast(I32), 0)
         nc.sync.dma_start(left_list[:], offs)
-        for q in range(4):
-            nc.sync.dma_start(scale_table[32 * q : 32 * q + 4, :].bitcast(I32), x_scales[0, 4 * q : 4 * q + 4, :].bitcast(I32))
+        for r in range(4):
+            nc.sync.dma_start(scale_table[r:P:32, :].bitcast(I32), x_scales[0, r:16:4, :].bitcast(I32))
         nc.sync.dma_start(right_list[:], right)
         nc.sync.dma_start(c_raw[:], cT.rearrange("(p j) m -> p j m", j=PACK))
         nc.sync.dma_start(word_table[:].bitcast(I32), x_words[0].rearrange("p c b -> p (c b)").bitcast(I32))

@@ -13,11 +13,14 @@ U16 = mybir.dt.uint16
 U8 = mybir.dt.uint8
 FP8X4 = mybir.dt.float8_e4m3fn_x4
 ALU = mybir.AluOpType
+ACT = mybir.ActivationFunctionType
 
 P = 128
 PACK = 4
 HALF = 128
 RUN = 4
+VECTOR_COLS = 64
+AREA_SPAN = RUN * (PACK - 1) + 1
 
 
 def tile_picked_yrus_upw_p_kernel(tc, x_words, x_scales, cT, area, qm, cur, offs, right, out):
@@ -31,9 +34,10 @@ def tile_picked_yrus_upw_p_kernel(tc, x_words, x_scales, cT, area, qm, cur, offs
         right_list = lists.tile([P, S // 16], U16, name="right_list")
         scale_table = sb.tile([P, T], U8, name="scale_table", align_bytes=64)
         word_table = sb.tile([P, T], U32, name="word_table", align_bytes=64)
-        c_raw = sb.tile([P, PACK, N], F32, name="c_raw")
-        q_raw = sb.tile([P, PACK, R], F32, name="q_raw", tag="q_raw_then_left")
-        area_sb = sb.tile([P, PACK], F32, name="area_sb")
+        c_raw = sb.tile([P, PACK, N], F32, name="c_raw", tag="c_raw_then_words", align_bytes=64)
+        q_low = sb.tile([P, 2, R], F32, name="q_low", tag="q_low_then_left", align_bytes=64)
+        q_high = sb.tile([P, 2, R], F32, name="q_high")
+        area_sb = sb.tile([P, AREA_SPAN], F32, name="area_sb")
         cur_sb = sb.tile([P, R // P, N], F32, name="cur_sb")
 
         nc.vector.memset(scale_table[:].bitcast(I32), 0)
@@ -43,13 +47,12 @@ def tile_picked_yrus_upw_p_kernel(tc, x_words, x_scales, cT, area, qm, cur, offs
         nc.sync.dma_start(right_list[:], right)
         nc.sync.dma_start(c_raw[:], cT.rearrange("(p j) m -> p j m", j=PACK))
         nc.sync.dma_start(word_table[:].bitcast(I32), x_words[0].rearrange("p c b -> p (c b)").bitcast(I32))
-        qm_dealt = qm.rearrange("(c j i) r -> i c j r", j=PACK, i=RUN)
-        area_dealt = area.rearrange("(c j i) o -> i c (j o)", j=PACK, i=RUN)
+        area_groups = area.rearrange("(g s) o -> g (s o)", s=PACK * RUN)
         for i in range(RUN):
-            nc.sync.dma_start(q_raw[i:P:RUN, :, :], qm_dealt[i])
-        with nc.allow_non_contiguous_dma(reason="one area a face"):
-            for i in range(RUN):
-                nc.sync.dma_start(area_sb[i:P:RUN, :], area_dealt[i])
+            nc.sync.dma_start(area_sb[i:P:RUN, :], area_groups[:, i : i + AREA_SPAN])
+        qm_view = qm.rearrange("(g j i) r -> j g i r", j=PACK, i=RUN)
+        for j in range(PACK):
+            nc.sync.dma_start((q_low, q_high)[j // 2][:, j % 2, :], qm_view[j])
         nc.sync.dma_start(cur_sb[:], cur.rearrange("(e p) m -> p e m", p=P))
 
         picked_scales = sb.tile([P, 2, S], U8, name="picked_scales", align_bytes=64)
@@ -57,75 +60,130 @@ def tile_picked_yrus_upw_p_kernel(tc, x_words, x_scales, cT, area, qm, cur, offs
         both_lists = (left_list, right_list)
         for side in range(2):
             nc.vector.tensor_copy(picked_scales[:, side, :], scale_table[:].indirect(both_lists[side][:]))
+        nc.vector.tensor_copy(
+            dealt_scales[:].bitcast(I32).rearrange("q s (j c) -> q s j c", j=PACK),
+            picked_scales[:].bitcast(I32).rearrange("q s (c j) -> q s j c", j=PACK),
+        )
 
-        c_bf = sb.tile([P, N, PACK], BF16, name="c_bf", tag="c_bf_then_words", align_bytes=64)
+        c_bf = sb.tile([P, N, PACK], BF16, name="c_bf", align_bytes=64)
         c_codes = sb.tile([P, N], U32, name="c_codes", align_bytes=64)
         c_scales = sb.tile([P, N], U8, name="c_scales", align_bytes=64)
         nc.scalar.copy(c_bf[:], c_raw[:].rearrange("p j m -> p m j"))
         nc.vector.quantize_mx(out=c_codes[:].bitcast(FP8X4), scales=c_scales[:], in_=c_bf[:].rearrange("p m j -> p (m j)"))
 
-        words = sb.tile([P, 2, S], U32, name="words", tag="c_bf_then_words", align_bytes=64)
-        states = []
-        for side in range(2):
-            nc.vector.tensor_copy(
-                dealt_scales[:, side, :].bitcast(I32).rearrange("q (j c) -> q j c", j=PACK),
-                picked_scales[:, side, :].bitcast(I32).rearrange("q (c j) -> q j c", j=PACK),
-            )
-            nc.vector.tensor_copy(words[:, side, :].rearrange("q (j c i) -> q c j i", j=PACK, i=RUN), word_table[:].indirect(both_lists[side][:]))
-            banks = []
-            for h in range(N // HALF):
-                cols = slice(h * HALF, (h + 1) * HALF)
-                bank = ps.tile([P, PACK, HALF], F32, name=f"state{side}{h}")
-                for j in range(PACK):
-                    faces = slice(j * P, (j + 1) * P)
-                    nc.tensor.matmul_mx(
-                        out=bank[:, j, :],
-                        lhsT=words[:, side, faces].bitcast(FP8X4),
-                        lhsT_scale=dealt_scales[:, side, faces],
-                        rhs=c_codes[:, cols].bitcast(FP8X4),
-                        rhs_scale=c_scales[:, cols],
-                        start=True,
-                        stop=True,
-                    )
-                banks.append(bank)
-            states.append(banks)
+        area_size = sb.tile([P, PACK], F32, name="area_size")
+        last_size = sb.tile([P, 1], F32, name="last_size", tag="last_size_then_fa", align_bytes=64)
+        left_size = sb.tile([P, PACK - 1], F32, name="left_size", tag="left_size_then_q_bf", align_bytes=64)
+        area_sign0 = sb.tile([P, PACK], F32, name="area_sign0")
+        sign_low = sb.tile([P, 2], F32, name="sign_low", tag="sign_low_then_left", align_bytes=64)
+        sign_high = sb.tile([P, 2], F32, name="sign_high")
+        nc.scalar.activation(area_sign0[:], area_sb[:, 0:AREA_SPAN:RUN], ACT.Sign)
+        nc.scalar.activation(left_size[:], area_sb[:, 0 : AREA_SPAN - 1 : RUN], ACT.Abs)
+        nc.scalar.activation(sign_low[:], area_sign0[:, 0:2], ACT.Sign, scale=2.0, bias=1.0)
+        nc.scalar.activation(sign_high[:], area_sign0[:, 2:4], ACT.Sign, scale=2.0, bias=1.0)
+        nc.scalar.activation(area_size[:], area_sb[:, 0:AREA_SPAN:RUN], ACT.Abs)
+        nc.scalar.activation(last_size[:], area_sb[:, AREA_SPAN - 1 : AREA_SPAN], ACT.Abs)
 
-        q_bf = sb.tile([P, R, PACK], BF16, name="q_bf", tag="q_bf_then_flux", align_bytes=64)
-        q_codes = sb.tile([P, R], U32, name="q_codes", align_bytes=64)
-        q_scales = sb.tile([P, R], U8, name="q_scales", align_bytes=64)
-        nc.scalar.copy(q_bf[:], q_raw[:].rearrange("p j r -> p r j"))
-        nc.vector.quantize_mx(out=q_codes[:].bitcast(FP8X4), scales=q_scales[:], in_=q_bf[:].rearrange("p r j -> p (r j)"))
+        words = sb.tile([P, 2, S], U32, name="words", tag="c_raw_then_words", align_bytes=64)
+        for side in range(2):
+            nc.vector.tensor_copy(words[:, side, :].rearrange("q (j c i) -> q c j i", j=PACK, i=RUN), word_table[:].indirect(both_lists[side][:]))
+
+        def first_product(bank, side, j, cols):
+            faces = slice(j * P, (j + 1) * P)
+            nc.tensor.matmul_mx(
+                out=bank,
+                lhsT=words[:, side, faces].bitcast(FP8X4),
+                lhsT_scale=dealt_scales[:, side, faces],
+                rhs=c_codes[:, cols].bitcast(FP8X4),
+                rhs_scale=c_scales[:, cols],
+                start=True,
+                stop=True,
+            )
 
         halves = range(N // HALF)
-        left_sb = sb.tile([P, N, PACK], F32, name="left_sb", tag="q_raw_then_left")
-        flux = sb.tile([P, N, PACK], F32, name="flux", tag="q_bf_then_flux", align_bytes=64)
+        cols = [slice(h * HALF, (h + 1) * HALF) for h in halves]
+        left_banks = [ps.tile([P, N], F32, name=f"left{j}", tag=f"bank{j}") for j in range(PACK)]
+        first_banks = [ps.tile([P, HALF], F32, name=f"right{j}", tag=f"bank{PACK + j}") for j in range(PACK)]
+        for j in range(PACK):
+            first_product(left_banks[j][:], 0, j, slice(0, N))
+
+        q_signed = sb.tile([P, PACK, R], BF16, name="q_signed", align_bytes=64)
+        for j in range(2):
+            nc.scalar.activation(q_signed[:, j, :], q_low[:, j, :], ACT.Copy, scale=sign_low[:, j : j + 1])
+        for j in range(2):
+            nc.vector.tensor_scalar(q_signed[:, 2 + j, :], q_high[:, j, :], sign_high[:, j : j + 1], None, ALU.mult)
+
+        left_pairs = [
+            sb.tile([P, 2, N], F32, name="left_low", tag="q_low_then_left", align_bytes=64),
+            sb.tile([P, 2, N], F32, name="left_high", tag="sign_low_then_left", align_bytes=64),
+        ]
+        for j in range(PACK):
+            size = left_size[:, j : j + 1] if j < PACK - 1 else last_size[:]
+            nc.scalar.activation(left_pairs[j // 2][:, j % 2, :], left_banks[j][:], ACT.Copy, scale=size)
+
+        q_bf = [
+            sb.tile([P, P, PACK], BF16, name="q_bf0", align_bytes=64),
+            sb.tile([P, P, PACK], BF16, name="q_bf1", tag="left_size_then_q_bf", align_bytes=64),
+        ]
+        q_codes = sb.tile([P, R // P, P], U32, name="q_codes", tag="q_low_then_left", align_bytes=64)
+        q_scales = [sb.tile([P, P], U8, name=f"q_scales{e}", align_bytes=64) for e in range(R // P)]
+        fa_flat = [
+            sb.tile([P, PACK, HALF], BF16, name="fa_flat0", align_bytes=64),
+            sb.tile([P, PACK, HALF], BF16, name="fa_flat1", tag="last_size_then_fa", align_bytes=64),
+        ]
         fa_bf = [sb.tile([P, HALF, PACK], BF16, name=f"fa_bf{h}", align_bytes=64) for h in halves]
         fa_codes = [sb.tile([P, HALF], U32, name=f"fa_codes{h}", align_bytes=64) for h in halves]
         fa_scales = [sb.tile([P, HALF], U8, name=f"fa_scales{h}", align_bytes=64) for h in halves]
         result = [sb.tile([P, R // P, HALF], F32, name=f"result{h}") for h in halves]
-        cols = [slice(h * HALF, (h + 1) * HALF) for h in halves]
+        rows = [slice(e * P, (e + 1) * P) for e in range(R // P)]
+
+        nc.vector.tensor_copy(q_bf[0][:], q_signed[:, :, rows[0]].rearrange("p j r -> p r j"))
+        nc.scalar.copy(q_bf[1][:], q_signed[:, :, rows[1]].rearrange("p j r -> p r j"))
+        second_banks = [ps.tile([P, HALF], F32, name=f"right_second{j}", tag=f"bank{j}") for j in range(PACK)]
+        right_states = [[bank[:] for bank in first_banks], [bank[:] for bank in second_banks]]
+        for h in halves:
+            for j in range(PACK):
+                first_product(right_states[h][j], 1, j, cols[h])
+
+        def quantize_q(e):
+            nc.vector.quantize_mx(out=q_codes[:, e, :].bitcast(FP8X4), scales=q_scales[e][:], in_=q_bf[e][:].rearrange("p r j -> p (r j)"))
 
         for h in halves:
-            nc.scalar.copy(left_sb[:, cols[h], :], states[0][h][:].rearrange("p j m -> p m j"))
-        for h in halves:
-            nc.vector.tensor_tensor(flux[:, cols[h], :], states[1][h][:].rearrange("p j m -> p m j"), left_sb[:, cols[h], :], ALU.min)
-        for h in halves:
-            nc.vector.tensor_tensor(fa_bf[h][:], flux[:, cols[h], :], area_sb[:].unsqueeze(1).to_broadcast([P, HALF, PACK]), ALU.mult)
-        for h in halves:
-            nc.vector.quantize_mx(out=fa_codes[h][:].bitcast(FP8X4), scales=fa_scales[h][:], in_=fa_bf[h][:].rearrange("p m j -> p (m j)"))
-        out_view = out.rearrange("(e p) m -> p e m", p=P)
-        for h in halves:
-            acc = ps.tile([P, R // P, HALF], F32, name=f"acc{h}")
-            for e in range(R // P):
-                rows = slice(e * P, (e + 1) * P)
-                nc.tensor.matmul_mx(
-                    out=acc[:, e, :],
-                    lhsT=q_codes[:, rows].bitcast(FP8X4),
-                    lhsT_scale=q_scales[:, rows],
-                    rhs=fa_codes[h][:].bitcast(FP8X4),
-                    rhs_scale=fa_scales[h][:],
-                    start=True,
-                    stop=True,
+            for j in range(PACK):
+                nc.vector.scalar_tensor_tensor(
+                    fa_flat[h][:, j, :], right_states[h][j], area_size[:, j : j + 1], left_pairs[j // 2][:, j % 2, cols[h]], ALU.mult, ALU.min
                 )
-            nc.vector.scalar_tensor_tensor(result[h][:], acc[:], -0.5, cur_sb[:, :, cols[h]], ALU.mult, ALU.add)
-            (nc.sync, nc.scalar)[h].dma_start(out_view[:, :, cols[h]], result[h][:])
+        nc.scalar.copy(fa_bf[0][:], fa_flat[0][:].rearrange("p j m -> p m j"))
+        for e in range(R // P):
+            quantize_q(e)
+
+        def quantize_fa(h):
+            nc.vector.quantize_mx(out=fa_codes[h][:].bitcast(FP8X4), scales=fa_scales[h][:], in_=fa_bf[h][:].rearrange("p m j -> p (m j)"))
+
+        quantize_fa(0)
+        nc.vector.tensor_copy(fa_bf[1][:, :VECTOR_COLS, :], fa_flat[1][:, :, :VECTOR_COLS].rearrange("p j m -> p m j"))
+        nc.scalar.copy(fa_bf[1][:, VECTOR_COLS:, :], fa_flat[1][:, :, VECTOR_COLS:].rearrange("p j m -> p m j"))
+        quantize_fa(1)
+
+        def second_product(bank, e, h):
+            nc.tensor.matmul_mx(
+                out=bank,
+                lhsT=q_codes[:, e, :].bitcast(FP8X4),
+                lhsT_scale=q_scales[e][:],
+                rhs=fa_codes[h][:].bitcast(FP8X4),
+                rhs_scale=fa_scales[h][:],
+                start=True,
+                stop=True,
+            )
+
+        out_view = out.rearrange("(e p) m -> p e m", p=P)
+        acc = ps.tile([P, R // P, HALF], F32, name="acc", tag=f"bank{PACK}")
+        for e in range(R // P):
+            second_product(acc[:, e, :], e, 0)
+        nc.vector.scalar_tensor_tensor(result[0][:], acc[:], -0.5, cur_sb[:, :, cols[0]], ALU.mult, ALU.add)
+        nc.sync.dma_start(out_view[:, :, cols[0]], result[0][:])
+        for e in range(R // P):
+            last_acc = ps.tile([P, HALF], F32, name=f"last_acc{e}", tag=f"bank{PACK + 1 + e}")
+            second_product(last_acc[:], e, 1)
+            nc.vector.scalar_tensor_tensor(result[1][:, e, :], last_acc[:], -0.5, cur_sb[:, e, cols[1]], ALU.mult, ALU.add)
+            (nc.scalar, nc.sync)[e].dma_start(out_view[:, e, cols[1]], result[1][:, e, :])

@@ -23,6 +23,10 @@ VECTOR_COLS = 64
 AREA_SPAN = RUN * (PACK - 1) + 1
 
 
+def interleave(copy, dst, src, step):
+    copy(dst.rearrange("p (c i) j -> p c j i", i=step), src.rearrange("p j (c i) -> p c j i", i=step))
+
+
 def tile_picked_yrus_upw_p_kernel(tc, x_words, x_scales, cT, area, qm, cur, offs, right, out):
     nc = tc.nc
     with ExitStack() as ctx:
@@ -35,8 +39,8 @@ def tile_picked_yrus_upw_p_kernel(tc, x_words, x_scales, cT, area, qm, cur, offs
         scale_table = sb.tile([P, T], U8, name="scale_table", align_bytes=64)
         word_table = sb.tile([P, T], U32, name="word_table", align_bytes=64)
         c_raw = sb.tile([P, PACK, N], F32, name="c_raw", tag="c_raw_then_words", align_bytes=64)
-        q_low = sb.tile([P, 2, R], F32, name="q_low", tag="q_low_then_left", align_bytes=64)
-        q_high = sb.tile([P, 2, R], F32, name="q_high")
+        q_low = sb.tile([P, PACK - 1, R], F32, name="q_low", tag="q_low_then_left", align_bytes=64)
+        q_high = sb.tile([P, R], F32, name="q_high")
         area_sb = sb.tile([P, AREA_SPAN], F32, name="area_sb")
         cur_sb = sb.tile([P, R // P, N], F32, name="cur_sb")
 
@@ -51,8 +55,9 @@ def tile_picked_yrus_upw_p_kernel(tc, x_words, x_scales, cT, area, qm, cur, offs
         for i in range(RUN):
             nc.sync.dma_start(area_sb[i:P:RUN, :], area_groups[:, i : i + AREA_SPAN])
         qm_view = qm.rearrange("(g j i) r -> j g i r", j=PACK, i=RUN)
-        for j in range(PACK):
-            nc.sync.dma_start((q_low, q_high)[j // 2][:, j % 2, :], qm_view[j])
+        for j in range(PACK - 1):
+            nc.sync.dma_start(q_low[:, j, :], qm_view[j])
+        nc.sync.dma_start(q_high[:], qm_view[PACK - 1])
         nc.sync.dma_start(cur_sb[:], cur.rearrange("(e p) m -> p e m", p=P))
 
         picked_scales = sb.tile([P, 2, S], U8, name="picked_scales", align_bytes=64)
@@ -68,19 +73,19 @@ def tile_picked_yrus_upw_p_kernel(tc, x_words, x_scales, cT, area, qm, cur, offs
         c_bf = sb.tile([P, N, PACK], BF16, name="c_bf", align_bytes=64)
         c_codes = sb.tile([P, N], U32, name="c_codes", align_bytes=64)
         c_scales = sb.tile([P, N], U8, name="c_scales", align_bytes=64)
-        nc.scalar.copy(c_bf[:], c_raw[:].rearrange("p j m -> p m j"))
+        interleave(nc.scalar.copy, c_bf[:], c_raw[:], 2)
         nc.vector.quantize_mx(out=c_codes[:].bitcast(FP8X4), scales=c_scales[:], in_=c_bf[:].rearrange("p m j -> p (m j)"))
 
         area_size = sb.tile([P, PACK], F32, name="area_size")
         last_size = sb.tile([P, 1], F32, name="last_size", tag="last_size_then_fa", align_bytes=64)
         left_size = sb.tile([P, PACK - 1], F32, name="left_size", tag="left_size_then_q_bf", align_bytes=64)
         area_sign0 = sb.tile([P, PACK], F32, name="area_sign0")
-        sign_low = sb.tile([P, 2], F32, name="sign_low", tag="sign_low_then_left", align_bytes=64)
-        sign_high = sb.tile([P, 2], F32, name="sign_high")
+        sign_low = sb.tile([P, PACK - 1], F32, name="sign_low", tag="sign_low_then_left", align_bytes=64)
+        sign_high = sb.tile([P, 1], F32, name="sign_high")
         nc.scalar.activation(area_sign0[:], area_sb[:, 0:AREA_SPAN:RUN], ACT.Sign)
         nc.scalar.activation(left_size[:], area_sb[:, 0 : AREA_SPAN - 1 : RUN], ACT.Abs)
-        nc.scalar.activation(sign_low[:], area_sign0[:, 0:2], ACT.Sign, scale=2.0, bias=1.0)
-        nc.scalar.activation(sign_high[:], area_sign0[:, 2:4], ACT.Sign, scale=2.0, bias=1.0)
+        nc.scalar.activation(sign_low[:], area_sign0[:, : PACK - 1], ACT.Sign, scale=2.0, bias=1.0)
+        nc.scalar.activation(sign_high[:], area_sign0[:, PACK - 1 :], ACT.Sign, scale=2.0, bias=1.0)
         nc.scalar.activation(area_size[:], area_sb[:, 0:AREA_SPAN:RUN], ACT.Abs)
         nc.scalar.activation(last_size[:], area_sb[:, AREA_SPAN - 1 : AREA_SPAN], ACT.Abs)
 
@@ -108,10 +113,9 @@ def tile_picked_yrus_upw_p_kernel(tc, x_words, x_scales, cT, area, qm, cur, offs
             first_product(left_banks[j][:], 0, j, slice(0, N))
 
         q_signed = sb.tile([P, PACK, R], BF16, name="q_signed", align_bytes=64)
-        for j in range(2):
+        for j in range(PACK - 1):
             nc.scalar.activation(q_signed[:, j, :], q_low[:, j, :], ACT.Copy, scale=sign_low[:, j : j + 1])
-        for j in range(2):
-            nc.vector.tensor_scalar(q_signed[:, 2 + j, :], q_high[:, j, :], sign_high[:, j : j + 1], None, ALU.mult)
+        nc.vector.tensor_scalar(q_signed[:, PACK - 1, :], q_high[:], sign_high[:], None, ALU.mult)
 
         left_pairs = [
             sb.tile([P, 2, N], F32, name="left_low", tag="q_low_then_left", align_bytes=64),
@@ -137,8 +141,8 @@ def tile_picked_yrus_upw_p_kernel(tc, x_words, x_scales, cT, area, qm, cur, offs
         result = [sb.tile([P, R // P, HALF], F32, name=f"result{h}") for h in halves]
         rows = [slice(e * P, (e + 1) * P) for e in range(R // P)]
 
-        nc.vector.tensor_copy(q_bf[0][:], q_signed[:, :, rows[0]].rearrange("p j r -> p r j"))
-        nc.scalar.copy(q_bf[1][:], q_signed[:, :, rows[1]].rearrange("p j r -> p r j"))
+        interleave(nc.vector.tensor_copy, q_bf[0][:], q_signed[:, :, rows[0]], 4)
+        interleave(nc.scalar.copy, q_bf[1][:], q_signed[:, :, rows[1]], 4)
         second_banks = [ps.tile([P, HALF], F32, name=f"right_second{j}", tag=f"bank{j}") for j in range(PACK)]
         right_states = [[bank[:] for bank in first_banks], [bank[:] for bank in second_banks]]
         for h in halves:
@@ -153,7 +157,7 @@ def tile_picked_yrus_upw_p_kernel(tc, x_words, x_scales, cT, area, qm, cur, offs
                 nc.vector.scalar_tensor_tensor(
                     fa_flat[h][:, j, :], right_states[h][j], area_size[:, j : j + 1], left_pairs[j // 2][:, j % 2, cols[h]], ALU.mult, ALU.min
                 )
-        nc.scalar.copy(fa_bf[0][:], fa_flat[0][:].rearrange("p j m -> p m j"))
+        interleave(nc.scalar.copy, fa_bf[0][:], fa_flat[0][:], 4)
         for e in range(R // P):
             quantize_q(e)
 
@@ -161,8 +165,8 @@ def tile_picked_yrus_upw_p_kernel(tc, x_words, x_scales, cT, area, qm, cur, offs
             nc.vector.quantize_mx(out=fa_codes[h][:].bitcast(FP8X4), scales=fa_scales[h][:], in_=fa_bf[h][:].rearrange("p m j -> p (m j)"))
 
         quantize_fa(0)
-        nc.vector.tensor_copy(fa_bf[1][:, :VECTOR_COLS, :], fa_flat[1][:, :, :VECTOR_COLS].rearrange("p j m -> p m j"))
-        nc.scalar.copy(fa_bf[1][:, VECTOR_COLS:, :], fa_flat[1][:, :, VECTOR_COLS:].rearrange("p j m -> p m j"))
+        interleave(nc.vector.tensor_copy, fa_bf[1][:, :VECTOR_COLS, :], fa_flat[1][:, :, :VECTOR_COLS], 4)
+        interleave(nc.scalar.copy, fa_bf[1][:, VECTOR_COLS:, :], fa_flat[1][:, :, VECTOR_COLS:], 4)
         quantize_fa(1)
 
         def second_product(bank, e, h):

@@ -19,7 +19,8 @@ P = 128
 PACK = 4
 HALF = 128
 RUN = 4
-VECTOR_COLS = 64
+EARLY_COLS = 512
+VECTOR_COLS = 48
 AREA_SPAN = RUN * (PACK - 1) + 1
 
 
@@ -32,13 +33,14 @@ def tile_picked_yrus_upw_p_kernel(tc, x_words, x_scales, cT, area, qm, cur, offs
     with ExitStack() as ctx:
         lists = ctx.enter_context(tc.tile_pool(name="lists", bufs=1))
         sb = ctx.enter_context(tc.tile_pool(name="sb", bufs=1))
+        shared = ctx.enter_context(tc.tile_pool(name="shared", bufs=1))
         ps = ctx.enter_context(tc.psum_pool(name="ps", bufs=1))
 
         left_list = lists.tile([P, S // 16], U16, name="left_list")
         right_list = lists.tile([P, S // 16], U16, name="right_list")
         scale_table = sb.tile([P, T], U8, name="scale_table", align_bytes=64)
         word_table = sb.tile([P, T], U32, name="word_table", align_bytes=64)
-        c_raw = sb.tile([P, PACK, N], F32, name="c_raw", tag="c_raw_then_words", align_bytes=64)
+        c_raw = shared.tile([P, PACK, N], F32, name="c_raw", offset=0, align_bytes=64)
         q_low = sb.tile([P, PACK - 1, R], F32, name="q_low", tag="q_low_then_left", align_bytes=64)
         q_high = sb.tile([P, R], F32, name="q_high")
         area_sb = sb.tile([P, AREA_SPAN], F32, name="area_sb")
@@ -46,11 +48,13 @@ def tile_picked_yrus_upw_p_kernel(tc, x_words, x_scales, cT, area, qm, cur, offs
 
         nc.vector.memset(scale_table[:].bitcast(I32), 0)
         nc.sync.dma_start(left_list[:], offs)
+        words_view = x_words[0].rearrange("p c b -> p (c b)").bitcast(I32)
+        nc.sync.dma_start(word_table[:, :EARLY_COLS].bitcast(I32), words_view[:, :EARLY_COLS])
+        nc.sync.dma_start(right_list[:], right)
         for r in range(4):
             nc.sync.dma_start(scale_table[r:P:32, :].bitcast(I32), x_scales[0, r:16:4, :].bitcast(I32))
-        nc.sync.dma_start(right_list[:], right)
         nc.sync.dma_start(c_raw[:], cT.rearrange("(p j) m -> p j m", j=PACK))
-        nc.sync.dma_start(word_table[:].bitcast(I32), x_words[0].rearrange("p c b -> p (c b)").bitcast(I32))
+        nc.sync.dma_start(word_table[:, EARLY_COLS:].bitcast(I32), words_view[:, EARLY_COLS:])
         area_groups = area.rearrange("(g s) o -> g (s o)", s=PACK * RUN)
         for i in range(RUN):
             nc.sync.dma_start(area_sb[i:P:RUN, :], area_groups[:, i : i + AREA_SPAN])
@@ -61,20 +65,20 @@ def tile_picked_yrus_upw_p_kernel(tc, x_words, x_scales, cT, area, qm, cur, offs
         nc.sync.dma_start(cur_sb[:], cur.rearrange("(e p) m -> p e m", p=P))
 
         picked_scales = sb.tile([P, 2, S], U8, name="picked_scales", align_bytes=64)
-        dealt_scales = sb.tile([P, 2, S], U8, name="dealt_scales", align_bytes=64)
         both_lists = (left_list, right_list)
         for side in range(2):
             nc.vector.tensor_copy(picked_scales[:, side, :], scale_table[:].indirect(both_lists[side][:]))
-        nc.vector.tensor_copy(
-            dealt_scales[:].bitcast(I32).rearrange("q s (j c) -> q s j c", j=PACK),
-            picked_scales[:].bitcast(I32).rearrange("q s (c j) -> q s j c", j=PACK),
-        )
 
         c_bf = sb.tile([P, N, PACK], BF16, name="c_bf", align_bytes=64)
         c_codes = sb.tile([P, N], U32, name="c_codes", align_bytes=64)
         c_scales = sb.tile([P, N], U8, name="c_scales", align_bytes=64)
         interleave(nc.scalar.copy, c_bf[:], c_raw[:], 2)
         nc.vector.quantize_mx(out=c_codes[:].bitcast(FP8X4), scales=c_scales[:], in_=c_bf[:].rearrange("p m j -> p (m j)"))
+        dealt_scales = shared.tile([P, PACK, 2, P], U8, name="dealt_scales", offset=0, align_bytes=64)
+        nc.vector.tensor_copy(
+            dealt_scales[:].bitcast(I32).rearrange("q j s (b c) -> q (s b) j c", c=4),
+            picked_scales[:].bitcast(I32).rearrange("q s (b c j) -> q (s b) j c", j=PACK, c=4),
+        )
 
         area_size = sb.tile([P, PACK], F32, name="area_size")
         last_size = sb.tile([P, 1], F32, name="last_size", tag="last_size_then_fa", align_bytes=64)
@@ -89,7 +93,7 @@ def tile_picked_yrus_upw_p_kernel(tc, x_words, x_scales, cT, area, qm, cur, offs
         nc.scalar.activation(area_size[:], area_sb[:, 0:AREA_SPAN:RUN], ACT.Abs)
         nc.scalar.activation(last_size[:], area_sb[:, AREA_SPAN - 1 : AREA_SPAN], ACT.Abs)
 
-        words = sb.tile([P, 2, S], U32, name="words", tag="c_raw_then_words", align_bytes=64)
+        words = shared.tile([P, 2, S], U32, name="words", offset=2 * S, align_bytes=64)
         for side in range(2):
             nc.vector.tensor_copy(words[:, side, :].rearrange("q (j c i) -> q c j i", j=PACK, i=RUN), word_table[:].indirect(both_lists[side][:]))
 
@@ -98,7 +102,7 @@ def tile_picked_yrus_upw_p_kernel(tc, x_words, x_scales, cT, area, qm, cur, offs
             nc.tensor.matmul_mx(
                 out=bank,
                 lhsT=words[:, side, faces].bitcast(FP8X4),
-                lhsT_scale=dealt_scales[:, side, faces],
+                lhsT_scale=dealt_scales[:, j, side, :],
                 rhs=c_codes[:, cols].bitcast(FP8X4),
                 rhs_scale=c_scales[:, cols],
                 start=True,

@@ -82,12 +82,12 @@ def tile_picked_yrus_upw_p_kernel(tc, x_words, x_scales, cT, area, qm, cur, offs
 
         area_size = sb.tile([P, PACK], F32, name="area_size")
         last_size = sb.tile([P, 1], F32, name="last_size", tag="last_size_then_fa", align_bytes=64)
-        left_size = sb.tile([P, PACK - 1], F32, name="left_size", tag="left_size_then_q_bf", align_bytes=64)
+        left_size = sb.tile([P, PACK - 2], F32, name="left_size", tag="left_size_then_q_bf", align_bytes=64)
         area_sign0 = sb.tile([P, PACK], F32, name="area_sign0")
         sign_low = sb.tile([P, PACK - 1], F32, name="sign_low", tag="sign_low_then_left", align_bytes=64)
         sign_high = sb.tile([P, 1], F32, name="sign_high")
         nc.scalar.activation(area_sign0[:], area_sb[:, 0:AREA_SPAN:RUN], ACT.Sign)
-        nc.scalar.activation(left_size[:], area_sb[:, 0 : AREA_SPAN - 1 : RUN], ACT.Abs)
+        nc.scalar.activation(left_size[:], area_sb[:, RUN : AREA_SPAN - 1 : RUN], ACT.Abs)
         nc.scalar.activation(sign_low[:], area_sign0[:, : PACK - 1], ACT.Sign, scale=2.0, bias=1.0)
         nc.scalar.activation(sign_high[:], area_sign0[:, PACK - 1 :], ACT.Sign, scale=2.0, bias=1.0)
         nc.scalar.activation(area_size[:], area_sb[:, 0:AREA_SPAN:RUN], ACT.Abs)
@@ -125,8 +125,9 @@ def tile_picked_yrus_upw_p_kernel(tc, x_words, x_scales, cT, area, qm, cur, offs
             sb.tile([P, 2, N], F32, name="left_low", tag="q_low_then_left", align_bytes=64),
             sb.tile([P, 2, N], F32, name="left_high", tag="sign_low_then_left", align_bytes=64),
         ]
-        for j in range(PACK):
-            size = left_size[:, j : j + 1] if j < PACK - 1 else last_size[:]
+        nc.vector.tensor_scalar(left_pairs[0][:, 0, :], left_banks[0][:], area_size[:, 0:1], None, ALU.mult)
+        for j in range(1, PACK):
+            size = left_size[:, j - 1 : j] if j < PACK - 1 else last_size[:]
             nc.scalar.activation(left_pairs[j // 2][:, j % 2, :], left_banks[j][:], ACT.Copy, scale=size)
 
         q_bf = [
@@ -145,7 +146,7 @@ def tile_picked_yrus_upw_p_kernel(tc, x_words, x_scales, cT, area, qm, cur, offs
         result = [sb.tile([P, R // P, HALF], F32, name=f"result{h}") for h in halves]
         rows = [slice(e * P, (e + 1) * P) for e in range(R // P)]
 
-        interleave(nc.vector.tensor_copy, q_bf[0][:], q_signed[:, :, rows[0]], 4)
+        nc.gpsimd.tensor_scalar(q_bf[0][:], q_signed[:, :, rows[0]].rearrange("p j r -> p r j"), 1.0, 0.0, ALU.mult, ALU.add)
         interleave(nc.scalar.copy, q_bf[1][:], q_signed[:, :, rows[1]], 4)
         second_banks = [ps.tile([P, HALF], F32, name=f"right_second{j}", tag=f"bank{j}") for j in range(PACK)]
         right_states = [[bank[:] for bank in first_banks], [bank[:] for bank in second_banks]]
@@ -162,8 +163,7 @@ def tile_picked_yrus_upw_p_kernel(tc, x_words, x_scales, cT, area, qm, cur, offs
                     fa_flat[h][:, j, :], right_states[h][j], area_size[:, j : j + 1], left_pairs[j // 2][:, j % 2, cols[h]], ALU.mult, ALU.min
                 )
         interleave(nc.scalar.copy, fa_bf[0][:], fa_flat[0][:], 4)
-        for e in range(R // P):
-            quantize_q(e)
+        quantize_q(1)
 
         def quantize_fa(h):
             nc.vector.quantize_mx(out=fa_codes[h][:].bitcast(FP8X4), scales=fa_scales[h][:], in_=fa_bf[h][:].rearrange("p m j -> p (m j)"))
@@ -171,6 +171,7 @@ def tile_picked_yrus_upw_p_kernel(tc, x_words, x_scales, cT, area, qm, cur, offs
         quantize_fa(0)
         interleave(nc.vector.tensor_copy, fa_bf[1][:, :VECTOR_COLS, :], fa_flat[1][:, :, :VECTOR_COLS], 4)
         interleave(nc.scalar.copy, fa_bf[1][:, VECTOR_COLS:, :], fa_flat[1][:, :, VECTOR_COLS:], 4)
+        quantize_q(0)
         quantize_fa(1)
 
         def second_product(bank, e, h):
@@ -185,13 +186,9 @@ def tile_picked_yrus_upw_p_kernel(tc, x_words, x_scales, cT, area, qm, cur, offs
             )
 
         out_view = out.rearrange("(e p) m -> p e m", p=P)
-        acc = ps.tile([P, R // P, HALF], F32, name="acc", tag=f"bank{PACK}")
-        for e in range(R // P):
-            second_product(acc[:, e, :], e, 0)
-        nc.vector.scalar_tensor_tensor(result[0][:], acc[:], -0.5, cur_sb[:, :, cols[0]], ALU.mult, ALU.add)
-        nc.sync.dma_start(out_view[:, :, cols[0]], result[0][:])
-        for e in range(R // P):
-            last_acc = ps.tile([P, HALF], F32, name=f"last_acc{e}", tag=f"bank{PACK + 1 + e}")
-            second_product(last_acc[:], e, 1)
-            nc.vector.scalar_tensor_tensor(result[1][:, e, :], last_acc[:], -0.5, cur_sb[:, e, cols[1]], ALU.mult, ALU.add)
-            (nc.scalar, nc.sync)[e].dma_start(out_view[:, e, cols[1]], result[1][:, e, :])
+        for h in halves:
+            for e in reversed(range(R // P)):
+                acc = ps.tile([P, HALF], F32, name=f"acc{h}{e}", tag=f"bank{PACK + 2 * h + e}")
+                second_product(acc[:], e, h)
+                nc.vector.scalar_tensor_tensor(result[h][:, e, :], acc[:], -0.5, cur_sb[:, e, cols[h]], ALU.mult, ALU.add)
+                (nc.scalar, nc.sync)[e].dma_start(out_view[:, e, cols[h]], result[h][:, e, :])

@@ -44,41 +44,58 @@ def tile_picked_yrus_upw_p_kernel(tc, x_words, x_scales, cT, area, qm, cur, offs
         q_low = sb.tile([P, PACK - 1, R], F32, name="q_low", tag="q_low_then_left", align_bytes=64)
         q_high = sb.tile([P, R], F32, name="q_high")
         area_sb = sb.tile([P, AREA_SPAN], F32, name="area_sb")
-        cur_sb = sb.tile([P, R // P, N], F32, name="cur_sb")
+        cur_sb = shared.tile([P, R // P, N], F32, name="cur_sb", offset=S, align_bytes=64)
 
         nc.vector.memset(scale_table[:].bitcast(I32), 0)
         nc.sync.dma_start(left_list[:], offs)
         words_view = x_words[0].rearrange("p c b -> p (c b)").bitcast(I32)
         nc.sync.dma_start(word_table[:, :EARLY_COLS].bitcast(I32), words_view[:, :EARLY_COLS])
-        nc.sync.dma_start(right_list[:], right)
-        for r in range(4):
-            nc.sync.dma_start(scale_table[r:P:32, :].bitcast(I32), x_scales[0, r:16:4, :].bitcast(I32))
-        nc.sync.dma_start(c_raw[:], cT.rearrange("(p j) m -> p j m", j=PACK))
-        nc.sync.dma_start(word_table[:, EARLY_COLS:].bitcast(I32), words_view[:, EARLY_COLS:])
         area_groups = area.rearrange("(g s) o -> g (s o)", s=PACK * RUN)
-        for i in range(RUN):
-            nc.sync.dma_start(area_sb[i:P:RUN, :], area_groups[:, i : i + AREA_SPAN])
+
+        def load_area(queue, i):
+            queue.dma_start(area_sb[i:P:RUN, :], area_groups[:, i : i + AREA_SPAN])
+
+        load_area(nc.sync, 0)
+        for r in range(2):
+            nc.sync.dma_start(scale_table[r:P:16, :].bitcast(I32), x_scales[0, r:16:2, :].bitcast(I32))
+        nc.sync.dma_start(c_raw[:], cT.rearrange("(p j) m -> p j m", j=PACK))
+        nc.sync.dma_start(right_list[:], right)
+        nc.sync.dma_start(word_table[:, EARLY_COLS:].bitcast(I32), words_view[:, EARLY_COLS:])
+        load_area(nc.sync, 1)
+        load_area(nc.gpsimd, 2)
+        load_area(nc.gpsimd, 3)
         qm_view = qm.rearrange("(g j i) r -> j g i r", j=PACK, i=RUN)
         for j in range(PACK - 1):
             nc.sync.dma_start(q_low[:, j, :], qm_view[j])
         nc.sync.dma_start(q_high[:], qm_view[PACK - 1])
-        nc.sync.dma_start(cur_sb[:], cur.rearrange("(e p) m -> p e m", p=P))
 
-        picked_scales = sb.tile([P, 2, S], U8, name="picked_scales", align_bytes=64)
+        picked_scales = [sb.tile([P, S], U8, name=f"picked_scales{side}", align_bytes=64) for side in range(2)]
+        dealt_scales = [
+            sb.tile([P, PACK, P], U8, name="dealt_left", align_bytes=64),
+            shared.tile([P, PACK, P], U8, name="dealt_right", offset=0, align_bytes=64),
+        ]
         both_lists = (left_list, right_list)
-        for side in range(2):
-            nc.vector.tensor_copy(picked_scales[:, side, :], scale_table[:].indirect(both_lists[side][:]))
+
+        def deal(side, queue):
+            nc.vector.tensor_copy(
+                dealt_scales[side][:].bitcast(I32).rearrange("q j (b c) -> q b j c", c=4),
+                picked_scales[side][:].bitcast(I32).rearrange("q (b c j) -> q b j c", j=PACK, c=4),
+            )
+            rows = dealt_scales[side][:].rearrange("q j p -> q (j p)").bitcast(I32)
+            for r in range(2):
+                queue.dma_start(rows[2 + r : P : 32, :], rows[16 + r : P : 32, :])
+
+        nc.vector.tensor_copy(picked_scales[0][:], scale_table[:].indirect(left_list[:]))
+        deal(0, nc.sync)
+        nc.vector.tensor_copy(picked_scales[1][:], scale_table[:].indirect(right_list[:]))
 
         c_bf = sb.tile([P, N, PACK], BF16, name="c_bf", align_bytes=64)
         c_codes = sb.tile([P, N], U32, name="c_codes", align_bytes=64)
         c_scales = sb.tile([P, N], U8, name="c_scales", align_bytes=64)
         interleave(nc.scalar.copy, c_bf[:], c_raw[:], 2)
         nc.vector.quantize_mx(out=c_codes[:].bitcast(FP8X4), scales=c_scales[:], in_=c_bf[:].rearrange("p m j -> p (m j)"))
-        dealt_scales = shared.tile([P, PACK, 2, P], U8, name="dealt_scales", offset=0, align_bytes=64)
-        nc.vector.tensor_copy(
-            dealt_scales[:].bitcast(I32).rearrange("q j s (b c) -> q (s b) j c", c=4),
-            picked_scales[:].bitcast(I32).rearrange("q s (b c j) -> q (s b) j c", j=PACK, c=4),
-        )
+        deal(1, nc.sync)
+        nc.sync.dma_start(cur_sb[:], cur.rearrange("(e p) m -> p e m", p=P))
 
         area_size = sb.tile([P, PACK], F32, name="area_size")
         last_size = sb.tile([P, 1], F32, name="last_size", tag="last_size_then_fa", align_bytes=64)
@@ -93,7 +110,7 @@ def tile_picked_yrus_upw_p_kernel(tc, x_words, x_scales, cT, area, qm, cur, offs
         nc.scalar.activation(area_size[:], area_sb[:, 0:AREA_SPAN:RUN], ACT.Abs)
         nc.scalar.activation(last_size[:], area_sb[:, AREA_SPAN - 1 : AREA_SPAN], ACT.Abs)
 
-        words = shared.tile([P, 2, S], U32, name="words", offset=2 * S, align_bytes=64)
+        words = shared.tile([P, 2, S], U32, name="words", offset=5 * S, align_bytes=64)
         for side in range(2):
             nc.vector.tensor_copy(words[:, side, :].rearrange("q (j c i) -> q c j i", j=PACK, i=RUN), word_table[:].indirect(both_lists[side][:]))
 
@@ -102,7 +119,7 @@ def tile_picked_yrus_upw_p_kernel(tc, x_words, x_scales, cT, area, qm, cur, offs
             nc.tensor.matmul_mx(
                 out=bank,
                 lhsT=words[:, side, faces].bitcast(FP8X4),
-                lhsT_scale=dealt_scales[:, j, side, :],
+                lhsT_scale=dealt_scales[side][:, j, :],
                 rhs=c_codes[:, cols].bitcast(FP8X4),
                 rhs_scale=c_scales[:, cols],
                 start=True,

@@ -41,10 +41,9 @@ def tile_picked_yrus_upw_p_kernel(tc, x_words, x_scales, cT, area, qm, cur, offs
         scale_table = sb.tile([P, T], U8, name="scale_table", align_bytes=64)
         word_table = sb.tile([P, T], U32, name="word_table", align_bytes=64)
         c_raw = shared.tile([P, PACK, N], F32, name="c_raw", offset=0, align_bytes=64)
-        q_low = sb.tile([P, PACK - 1, R], F32, name="q_low", tag="q_low_then_left", align_bytes=64)
         q_high = sb.tile([P, R], F32, name="q_high")
         area_sb = sb.tile([P, AREA_SPAN], F32, name="area_sb")
-        cur_sb = shared.tile([P, R // P, N], F32, name="cur_sb", offset=S, align_bytes=64)
+
 
         nc.vector.memset(scale_table[:].bitcast(I32), 0)
         nc.sync.dma_start(left_list[:], offs)
@@ -64,12 +63,11 @@ def tile_picked_yrus_upw_p_kernel(tc, x_words, x_scales, cT, area, qm, cur, offs
         load_area(nc.sync, 1)
         load_area(nc.gpsimd, 2)
         load_area(nc.gpsimd, 3)
-        qm_view = qm.rearrange("(g j i) r -> j g i r", j=PACK, i=RUN)
-        for j in range(PACK - 1):
-            nc.sync.dma_start(q_low[:, j, :], qm_view[j])
-        nc.sync.dma_start(q_high[:], qm_view[PACK - 1])
 
-        picked_scales = [sb.tile([P, S], U8, name=f"picked_scales{side}", align_bytes=64) for side in range(2)]
+        picked_scales = [
+            sb.tile([P, S], U8, name="picked_left", tag="q_low_then_left", align_bytes=64),
+            sb.tile([P, S], U8, name="picked_right", tag="picked_then_cur", align_bytes=64),
+        ]
         dealt_scales = [
             sb.tile([P, PACK, P], U8, name="dealt_left", align_bytes=64),
             shared.tile([P, PACK, P], U8, name="dealt_right", offset=0, align_bytes=64),
@@ -87,6 +85,11 @@ def tile_picked_yrus_upw_p_kernel(tc, x_words, x_scales, cT, area, qm, cur, offs
 
         nc.vector.tensor_copy(picked_scales[0][:], scale_table[:].indirect(left_list[:]))
         deal(0, nc.sync)
+        q_low = sb.tile([P, PACK - 1, R], F32, name="q_low", tag="q_low_then_left", align_bytes=64)
+        qm_view = qm.rearrange("(g j i) r -> j g i r", j=PACK, i=RUN)
+        for j in range(PACK - 1):
+            nc.sync.dma_start(q_low[:, j, :], qm_view[j])
+        nc.sync.dma_start(q_high[:], qm_view[PACK - 1])
         nc.vector.tensor_copy(picked_scales[1][:], scale_table[:].indirect(right_list[:]))
 
         c_bf = sb.tile([P, N, PACK], BF16, name="c_bf", align_bytes=64)
@@ -95,6 +98,7 @@ def tile_picked_yrus_upw_p_kernel(tc, x_words, x_scales, cT, area, qm, cur, offs
         interleave(nc.scalar.copy, c_bf[:], c_raw[:], 2)
         nc.vector.quantize_mx(out=c_codes[:].bitcast(FP8X4), scales=c_scales[:], in_=c_bf[:].rearrange("p m j -> p (m j)"))
         deal(1, nc.sync)
+        cur_sb = sb.tile([P, R // P, N], F32, name="cur_sb", tag="picked_then_cur", align_bytes=64)
         nc.sync.dma_start(cur_sb[:], cur.rearrange("(e p) m -> p e m", p=P))
 
         area_size = sb.tile([P, PACK], F32, name="area_size")
@@ -110,7 +114,7 @@ def tile_picked_yrus_upw_p_kernel(tc, x_words, x_scales, cT, area, qm, cur, offs
         nc.scalar.activation(area_size[:], area_sb[:, 0:AREA_SPAN:RUN], ACT.Abs)
         nc.scalar.activation(last_size[:], area_sb[:, AREA_SPAN - 1 : AREA_SPAN], ACT.Abs)
 
-        words = shared.tile([P, 2, S], U32, name="words", offset=5 * S, align_bytes=64)
+        words = shared.tile([P, 2, S], U32, name="words", offset=2 * S, align_bytes=64)
         for side in range(2):
             nc.vector.tensor_copy(words[:, side, :].rearrange("q (j c i) -> q c j i", j=PACK, i=RUN), word_table[:].indirect(both_lists[side][:]))
 

@@ -61,8 +61,8 @@ def tile_picked_yrus_upw_p_kernel(tc, x_words, x_scales, cT, area, qm, cur, offs
         nc.sync.dma_start(right_list[:], right)
         nc.sync.dma_start(word_table[:, EARLY_COLS:].bitcast(I32), words_view[:, EARLY_COLS:])
         load_area(nc.sync, 1)
-        load_area(nc.gpsimd, 2)
-        load_area(nc.gpsimd, 3)
+        load_area(nc.scalar, 2)
+        load_area(nc.scalar, 3)
 
         picked_scales = [
             sb.tile([P, S], U8, name="picked_left", tag="q_low_then_left", align_bytes=64),

@@ -19,8 +19,10 @@ P = 128
 PACK = 4
 HALF = 128
 RUN = 4
-EARLY_COLS = 512
+EARLY_COLS = 384
 VECTOR_COLS = 48
+SIGN_SCALE = 2.0**40
+SIGN_BIAS = 2.0**-120
 AREA_SPAN = RUN * (PACK - 1) + 1
 
 
@@ -39,16 +41,16 @@ def tile_picked_yrus_upw_p_kernel(tc, x_words, x_scales, cT, area, qm, cur, offs
         left_list = lists.tile([P, S // 16], U16, name="left_list")
         right_list = lists.tile([P, S // 16], U16, name="right_list")
         scale_table = sb.tile([P, T], U8, name="scale_table", align_bytes=64)
-        word_table = sb.tile([P, T], U32, name="word_table", align_bytes=64)
+        word_table = sb.tile([P, T], U32, name="word_table", tag="words_then_q_bf", align_bytes=64)
         c_raw = shared.tile([P, PACK, N], F32, name="c_raw", offset=0, align_bytes=64)
         q_high = sb.tile([P, R], F32, name="q_high")
         area_sb = sb.tile([P, AREA_SPAN], F32, name="area_sb")
 
 
         nc.vector.memset(scale_table[:].bitcast(I32), 0)
-        nc.sync.dma_start(left_list[:], offs)
         words_view = x_words[0].rearrange("p c b -> p (c b)").bitcast(I32)
         nc.sync.dma_start(word_table[:, :EARLY_COLS].bitcast(I32), words_view[:, :EARLY_COLS])
+        nc.sync.dma_start(left_list[:], offs)
         area_groups = area.rearrange("(g s) o -> g (s o)", s=PACK * RUN)
 
         def load_area(queue, i):
@@ -103,14 +105,10 @@ def tile_picked_yrus_upw_p_kernel(tc, x_words, x_scales, cT, area, qm, cur, offs
 
         area_size = sb.tile([P, PACK], F32, name="area_size")
         last_size = sb.tile([P, 1], F32, name="last_size", tag="last_size_then_fa", align_bytes=64)
-        left_size = sb.tile([P, PACK - 2], F32, name="left_size", tag="left_size_then_q_bf", align_bytes=64)
-        area_sign0 = sb.tile([P, PACK], F32, name="area_sign0")
         sign_low = sb.tile([P, PACK - 1], F32, name="sign_low", tag="sign_low_then_left", align_bytes=64)
         sign_high = sb.tile([P, 1], F32, name="sign_high")
-        nc.scalar.activation(area_sign0[:], area_sb[:, 0:AREA_SPAN:RUN], ACT.Sign)
-        nc.scalar.activation(left_size[:], area_sb[:, RUN : AREA_SPAN - 1 : RUN], ACT.Abs)
-        nc.scalar.activation(sign_low[:], area_sign0[:, : PACK - 1], ACT.Sign, scale=2.0, bias=1.0)
-        nc.scalar.activation(sign_high[:], area_sign0[:, PACK - 1 :], ACT.Sign, scale=2.0, bias=1.0)
+        nc.scalar.activation(sign_low[:], area_sb[:, 0 : AREA_SPAN - 1 : RUN], ACT.Sign, scale=SIGN_SCALE, bias=SIGN_BIAS)
+        nc.scalar.activation(sign_high[:], area_sb[:, AREA_SPAN - 1 : AREA_SPAN], ACT.Sign, scale=SIGN_SCALE, bias=SIGN_BIAS)
         nc.scalar.activation(area_size[:], area_sb[:, 0:AREA_SPAN:RUN], ACT.Abs)
         nc.scalar.activation(last_size[:], area_sb[:, AREA_SPAN - 1 : AREA_SPAN], ACT.Abs)
 
@@ -140,20 +138,19 @@ def tile_picked_yrus_upw_p_kernel(tc, x_words, x_scales, cT, area, qm, cur, offs
         q_signed = sb.tile([P, PACK, R], BF16, name="q_signed", align_bytes=64)
         for j in range(PACK - 1):
             nc.scalar.activation(q_signed[:, j, :], q_low[:, j, :], ACT.Copy, scale=sign_low[:, j : j + 1])
-        nc.vector.tensor_scalar(q_signed[:, PACK - 1, :], q_high[:], sign_high[:], None, ALU.mult)
+        nc.scalar.activation(q_signed[:, PACK - 1, :], q_high[:], ACT.Copy, scale=sign_high[:])
 
         left_pairs = [
             sb.tile([P, 2, N], F32, name="left_low", tag="q_low_then_left", align_bytes=64),
             sb.tile([P, 2, N], F32, name="left_high", tag="sign_low_then_left", align_bytes=64),
         ]
-        nc.vector.tensor_scalar(left_pairs[0][:, 0, :], left_banks[0][:], area_size[:, 0:1], None, ALU.mult)
-        for j in range(1, PACK):
-            size = left_size[:, j - 1 : j] if j < PACK - 1 else last_size[:]
+        for j in range(PACK):
+            size = area_size[:, j : j + 1] if j < PACK - 1 else last_size[:]
             nc.scalar.activation(left_pairs[j // 2][:, j % 2, :], left_banks[j][:], ACT.Copy, scale=size)
 
         q_bf = [
-            sb.tile([P, P, PACK], BF16, name="q_bf0", align_bytes=64),
-            sb.tile([P, P, PACK], BF16, name="q_bf1", tag="left_size_then_q_bf", align_bytes=64),
+            sb.tile([P, P, PACK], BF16, name="q_bf0", tag="words_then_q_bf", align_bytes=64),
+            sb.tile([P, P, PACK], BF16, name="q_bf1", align_bytes=64),
         ]
         q_codes = sb.tile([P, R // P, P], U32, name="q_codes", tag="q_low_then_left", align_bytes=64)
         q_scales = [sb.tile([P, P], U8, name=f"q_scales{e}", align_bytes=64) for e in range(R // P)]
@@ -168,7 +165,7 @@ def tile_picked_yrus_upw_p_kernel(tc, x_words, x_scales, cT, area, qm, cur, offs
         rows = [slice(e * P, (e + 1) * P) for e in range(R // P)]
 
         nc.gpsimd.tensor_scalar(q_bf[0][:], q_signed[:, :, rows[0]].rearrange("p j r -> p r j"), 1.0, 0.0, ALU.mult, ALU.add)
-        interleave(nc.scalar.copy, q_bf[1][:], q_signed[:, :, rows[1]], 4)
+        interleave(nc.vector.tensor_copy, q_bf[1][:], q_signed[:, :, rows[1]], 4)
         second_banks = [ps.tile([P, HALF], F32, name=f"right_second{j}", tag=f"bank{j}") for j in range(PACK)]
         right_states = [[bank[:] for bank in first_banks], [bank[:] for bank in second_banks]]
         for h in halves:

@@ -21,6 +21,8 @@ HALF = 128
 RUN = 4
 EARLY_COLS = 384
 VECTOR_COLS = 48
+WARM_ROWS = 32
+WARM_PASSES = 8
 SIGN_SCALE = 2.0**40
 SIGN_BIAS = 2.0**-120
 AREA_SPAN = RUN * (PACK - 1) + 1
@@ -100,6 +102,17 @@ def tile_picked_yrus_upw_p_kernel(tc, x_words, x_scales, cT, area, qm, cur, offs
         interleave(nc.scalar.copy, c_bf[:], c_raw[:], 2)
         nc.vector.quantize_mx(out=c_codes[:].bitcast(FP8X4), scales=c_scales[:], in_=c_bf[:].rearrange("p m j -> p (m j)"))
         deal(1, nc.sync)
+        warm = ps.tile([WARM_ROWS, HALF], F32, name="warm", tag=f"bank{2 * PACK - 1}")
+        for n in range(WARM_PASSES):
+            nc.tensor.matmul_mx(
+                out=warm[:],
+                lhsT=c_codes[:, :WARM_ROWS].bitcast(FP8X4),
+                lhsT_scale=c_scales[:, :WARM_ROWS],
+                rhs=c_codes[:, :HALF].bitcast(FP8X4),
+                rhs_scale=c_scales[:, :HALF],
+                start=True,
+                stop=True,
+            )
         cur_sb = sb.tile([P, R // P, N], F32, name="cur_sb", tag="picked_then_cur", align_bytes=64)
         nc.sync.dma_start(cur_sb[:], cur.rearrange("(e p) m -> p e m", p=P))
 

@@ -20,7 +20,7 @@ PACK = 4
 HALF = 128
 RUN = 4
 EARLY_COLS = 384
-VECTOR_COLS = 48
+VECTOR_COLS = 72
 WARM_ROWS = 32
 WARM_PASSES = 8
 SIGN_SCALE = 2.0**40
@@ -53,23 +53,23 @@ def tile_picked_yrus_upw_p_kernel(tc, x_words, x_scales, cT, area, qm, cur, offs
         words_view = x_words[0].rearrange("p c b -> p (c b)").bitcast(I32)
         nc.sync.dma_start(word_table[:, :EARLY_COLS].bitcast(I32), words_view[:, :EARLY_COLS])
         nc.sync.dma_start(left_list[:], offs)
+        nc.sync.dma_start(right_list[:], right)
         area_groups = area.rearrange("(g s) o -> g (s o)", s=PACK * RUN)
 
         def load_area(queue, i):
             queue.dma_start(area_sb[i:P:RUN, :], area_groups[:, i : i + AREA_SPAN])
 
-        load_area(nc.sync, 0)
         for r in range(2):
             nc.sync.dma_start(scale_table[r:P:16, :].bitcast(I32), x_scales[0, r:16:2, :].bitcast(I32))
         nc.sync.dma_start(c_raw[:], cT.rearrange("(p j) m -> p j m", j=PACK))
-        nc.sync.dma_start(right_list[:], right)
         nc.sync.dma_start(word_table[:, EARLY_COLS:].bitcast(I32), words_view[:, EARLY_COLS:])
+        load_area(nc.sync, 0)
         load_area(nc.sync, 1)
         load_area(nc.scalar, 2)
         load_area(nc.scalar, 3)
 
         picked_scales = [
-            sb.tile([P, S], U8, name="picked_left", tag="q_low_then_left", align_bytes=64),
+            sb.tile([P, S], U8, name="picked_left", align_bytes=64),
             sb.tile([P, S], U8, name="picked_right", tag="picked_then_cur", align_bytes=64),
         ]
         dealt_scales = [
@@ -87,14 +87,14 @@ def tile_picked_yrus_upw_p_kernel(tc, x_words, x_scales, cT, area, qm, cur, offs
             for r in range(2):
                 queue.dma_start(rows[2 + r : P : 32, :], rows[16 + r : P : 32, :])
 
-        nc.vector.tensor_copy(picked_scales[0][:], scale_table[:].indirect(left_list[:]))
-        deal(0, nc.sync)
         q_low = sb.tile([P, PACK - 1, R], F32, name="q_low", tag="q_low_then_left", align_bytes=64)
         qm_view = qm.rearrange("(g j i) r -> j g i r", j=PACK, i=RUN)
         for j in range(PACK - 1):
             nc.sync.dma_start(q_low[:, j, :], qm_view[j])
         nc.sync.dma_start(q_high[:], qm_view[PACK - 1])
+        nc.vector.tensor_copy(picked_scales[0][:], scale_table[:].indirect(left_list[:]))
         nc.vector.tensor_copy(picked_scales[1][:], scale_table[:].indirect(right_list[:]))
+        deal(0, nc.sync)
 
         c_bf = sb.tile([P, N, PACK], BF16, name="c_bf", align_bytes=64)
         c_codes = sb.tile([P, N], U32, name="c_codes", align_bytes=64)

@@ -63,10 +63,8 @@ def tile_picked_yrus_upw_p_kernel(tc, x_words, x_scales, cT, area, qm, cur, offs
             nc.sync.dma_start(scale_table[r:P:16, :].bitcast(I32), x_scales[0, r:16:2, :].bitcast(I32))
         nc.sync.dma_start(c_raw[:], cT.rearrange("(p j) m -> p j m", j=PACK))
         nc.sync.dma_start(word_table[:, EARLY_COLS:].bitcast(I32), words_view[:, EARLY_COLS:])
-        load_area(nc.sync, 0)
-        load_area(nc.sync, 1)
-        load_area(nc.scalar, 2)
-        load_area(nc.scalar, 3)
+        for i in range(RUN):
+            load_area(nc.sync, i)
 
         picked_scales = [
             sb.tile([P, S], U8, name="picked_left", align_bytes=64),

from contextlib import ExitStack

import concourse.mybir as mybir

K, T, S, N, R = 512, 2048, 512, 256, 256
FLOPS = 2 * (2 * S * K * N + S * R * N)

F32 = mybir.dt.float32
BF16 = mybir.dt.bfloat16
I32 = mybir.dt.int32
U32 = mybir.dt.uint32
U16 = mybir.dt.uint16
U8 = mybir.dt.uint8
FP8X4 = mybir.dt.float8_e4m3fn_x4
ALU = mybir.AluOpType
ACT = mybir.ActivationFunctionType

P = 128
PACK = 4
HALF = 128
RUN = 4
EARLY_COLS = 384
VECTOR_COLS = 72
WARM_ROWS = 32
WARM_PASSES = 8
SIGN_SCALE = 2.0**40
SIGN_BIAS = 2.0**-120
AREA_SPAN = RUN * (PACK - 1) + 1


def interleave(copy, dst, src, step):
    copy(dst.rearrange("p (c i) j -> p c j i", i=step), src.rearrange("p j (c i) -> p c j i", i=step))


def tile_picked_yrus_upw_p_kernel(tc, x_words, x_scales, cT, area, qm, cur, offs, right, out):
    nc = tc.nc
    with ExitStack() as ctx:
        lists = ctx.enter_context(tc.tile_pool(name="lists", bufs=1))
        sb = ctx.enter_context(tc.tile_pool(name="sb", bufs=1))
        shared = ctx.enter_context(tc.tile_pool(name="shared", bufs=1))
        ps = ctx.enter_context(tc.psum_pool(name="ps", bufs=1))

        left_list = lists.tile([P, S // 16], U16, name="left_list")
        right_list = lists.tile([P, S // 16], U16, name="right_list")
        scale_table = sb.tile([P, T], U8, name="scale_table", align_bytes=64)
        word_table = sb.tile([P, T], U32, name="word_table", tag="words_then_q_bf", align_bytes=64)
        c_raw = shared.tile([P, PACK, N], F32, name="c_raw", offset=0, align_bytes=64)
        q_high = sb.tile([P, R], F32, name="q_high")
        area_sb = sb.tile([P, AREA_SPAN], F32, name="area_sb")


        nc.vector.memset(scale_table[:].bitcast(I32), 0)
        words_view = x_words[0].rearrange("p c b -> p (c b)").bitcast(I32)
        nc.sync.dma_start(word_table[:, :EARLY_COLS].bitcast(I32), words_view[:, :EARLY_COLS])
        nc.sync.dma_start(left_list[:], offs)
        nc.sync.dma_start(right_list[:], right)
        area_groups = area.rearrange("(g s) o -> g (s o)", s=PACK * RUN)

        def load_area(queue, i):
            queue.dma_start(area_sb[i:P:RUN, :], area_groups[:, i : i + AREA_SPAN])

        for r in range(2):
            nc.sync.dma_start(scale_table[r:P:16, :].bitcast(I32), x_scales[0, r:16:2, :].bitcast(I32))
        nc.sync.dma_start(c_raw[:], cT.rearrange("(p j) m -> p j m", j=PACK))
        nc.sync.dma_start(word_table[:, EARLY_COLS:].bitcast(I32), words_view[:, EARLY_COLS:])
        for i in range(RUN):
            load_area(nc.sync, i)

        picked_scales = [
            sb.tile([P, S], U8, name="picked_left", align_bytes=64),
            sb.tile([P, S], U8, name="picked_right", tag="picked_then_cur", align_bytes=64),
        ]
        dealt_scales = [
            sb.tile([P, PACK, P], U8, name="dealt_left", align_bytes=64),
            shared.tile([P, PACK, P], U8, name="dealt_right", offset=0, align_bytes=64),
        ]
        both_lists = (left_list, right_list)

        def deal(side, queue):
            nc.vector.tensor_copy(
                dealt_scales[side][:].bitcast(I32).rearrange("q j (b c) -> q b j c", c=4),
                picked_scales[side][:].bitcast(I32).rearrange("q (b c j) -> q b j c", j=PACK, c=4),
            )
            rows = dealt_scales[side][:].rearrange("q j p -> q (j p)").bitcast(I32)
            for r in range(2):
                queue.dma_start(rows[2 + r : P : 32, :], rows[16 + r : P : 32, :])

        q_low = sb.tile([P, PACK - 1, R], F32, name="q_low", tag="q_low_then_left", align_bytes=64)
        qm_view = qm.rearrange("(g j i) r -> j g i r", j=PACK, i=RUN)
        for j in range(PACK - 1):
            nc.sync.dma_start(q_low[:, j, :], qm_view[j])
        nc.sync.dma_start(q_high[:], qm_view[PACK - 1])
        nc.vector.tensor_copy(picked_scales[0][:], scale_table[:].indirect(left_list[:]))
        nc.vector.tensor_copy(picked_scales[1][:], scale_table[:].indirect(right_list[:]))
        deal(0, nc.sync)

        c_bf = sb.tile([P, N, PACK], BF16, name="c_bf", align_bytes=64)
        c_codes = sb.tile([P, N], U32, name="c_codes", align_bytes=64)
        c_scales = sb.tile([P, N], U8, name="c_scales", align_bytes=64)
        interleave(nc.scalar.copy, c_bf[:], c_raw[:], 2)
        nc.vector.quantize_mx(out=c_codes[:].bitcast(FP8X4), scales=c_scales[:], in_=c_bf[:].rearrange("p m j -> p (m j)"))
        deal(1, nc.sync)
        warm = ps.tile([WARM_ROWS, HALF], F32, name="warm", tag=f"bank{2 * PACK - 1}")
        for n in range(WARM_PASSES):
            nc.tensor.matmul_mx(
                out=warm[:],
                lhsT=c_codes[:, :WARM_ROWS].bitcast(FP8X4),
                lhsT_scale=c_scales[:, :WARM_ROWS],
                rhs=c_codes[:, :HALF].bitcast(FP8X4),
                rhs_scale=c_scales[:, :HALF],
                start=True,
                stop=True,
            )
        cur_sb = sb.tile([P, R // P, N], F32, name="cur_sb", tag="picked_then_cur", align_bytes=64)
        nc.sync.dma_start(cur_sb[:], cur.rearrange("(e p) m -> p e m", p=P))

        area_size = sb.tile([P, PACK], F32, name="area_size")
        last_size = sb.tile([P, 1], F32, name="last_size", tag="last_size_then_fa", align_bytes=64)
        sign_low = sb.tile([P, PACK - 1], F32, name="sign_low", tag="sign_low_then_left", align_bytes=64)
        sign_high = sb.tile([P, 1], F32, name="sign_high")
        nc.scalar.activation(sign_low[:], area_sb[:, 0 : AREA_SPAN - 1 : RUN], ACT.Sign, scale=SIGN_SCALE, bias=SIGN_BIAS)
        nc.scalar.activation(sign_high[:], area_sb[:, AREA_SPAN - 1 : AREA_SPAN], ACT.Sign, scale=SIGN_SCALE, bias=SIGN_BIAS)
        nc.scalar.activation(area_size[:], area_sb[:, 0:AREA_SPAN:RUN], ACT.Abs)
        nc.scalar.activation(last_size[:], area_sb[:, AREA_SPAN - 1 : AREA_SPAN], ACT.Abs)

        words = shared.tile([P, 2, S], U32, name="words", offset=2 * S, align_bytes=64)
        for side in range(2):
            nc.vector.tensor_copy(words[:, side, :].rearrange("q (j c i) -> q c j i", j=PACK, i=RUN), word_table[:].indirect(both_lists[side][:]))

        def first_product(bank, side, j, cols):
            faces = slice(j * P, (j + 1) * P)
            nc.tensor.matmul_mx(
                out=bank,
                lhsT=words[:, side, faces].bitcast(FP8X4),
                lhsT_scale=dealt_scales[side][:, j, :],
                rhs=c_codes[:, cols].bitcast(FP8X4),
                rhs_scale=c_scales[:, cols],
                start=True,
                stop=True,
            )

        halves = range(N // HALF)
        cols = [slice(h * HALF, (h + 1) * HALF) for h in halves]
        left_banks = [ps.tile([P, N], F32, name=f"left{j}", tag=f"bank{j}") for j in range(PACK)]
        first_banks = [ps.tile([P, HALF], F32, name=f"right{j}", tag=f"bank{PACK + j}") for j in range(PACK)]
        for j in range(PACK):
            first_product(left_banks[j][:], 0, j, slice(0, N))

        q_signed = sb.tile([P, PACK, R], BF16, name="q_signed", align_bytes=64)
        for j in range(PACK - 1):
            nc.scalar.activation(q_signed[:, j, :], q_low[:, j, :], ACT.Copy, scale=sign_low[:, j : j + 1])
        nc.scalar.activation(q_signed[:, PACK - 1, :], q_high[:], ACT.Copy, scale=sign_high[:])

        left_pairs = [
            sb.tile([P, 2, N], F32, name="left_low", tag="q_low_then_left", align_bytes=64),
            sb.tile([P, 2, N], F32, name="left_high", tag="sign_low_then_left", align_bytes=64),
        ]
        for j in range(PACK):
            size = area_size[:, j : j + 1] if j < PACK - 1 else last_size[:]
            nc.scalar.activation(left_pairs[j // 2][:, j % 2, :], left_banks[j][:], ACT.Copy, scale=size)

        q_bf = [
            sb.tile([P, P, PACK], BF16, name="q_bf0", tag="words_then_q_bf", align_bytes=64),
            sb.tile([P, P, PACK], BF16, name="q_bf1", align_bytes=64),
        ]
        q_codes = sb.tile([P, R // P, P], U32, name="q_codes", tag="q_low_then_left", align_bytes=64)
        q_scales = [sb.tile([P, P], U8, name=f"q_scales{e}", align_bytes=64) for e in range(R // P)]
        fa_flat = [
            sb.tile([P, PACK, HALF], BF16, name="fa_flat0", align_bytes=64),
            sb.tile([P, PACK, HALF], BF16, name="fa_flat1", tag="last_size_then_fa", align_bytes=64),
        ]
        fa_bf = [sb.tile([P, HALF, PACK], BF16, name=f"fa_bf{h}", align_bytes=64) for h in halves]
        fa_codes = [sb.tile([P, HALF], U32, name=f"fa_codes{h}", align_bytes=64) for h in halves]
        fa_scales = [sb.tile([P, HALF], U8, name=f"fa_scales{h}", align_bytes=64) for h in halves]
        result = [sb.tile([P, R // P, HALF], F32, name=f"result{h}") for h in halves]
        rows = [slice(e * P, (e + 1) * P) for e in range(R // P)]

        nc.gpsimd.tensor_scalar(q_bf[0][:], q_signed[:, :, rows[0]].rearrange("p j r -> p r j"), 1.0, 0.0, ALU.mult, ALU.add)
        interleave(nc.vector.tensor_copy, q_bf[1][:], q_signed[:, :, rows[1]], 4)
        second_banks = [ps.tile([P, HALF], F32, name=f"right_second{j}", tag=f"bank{j}") for j in range(PACK)]
        right_states = [[bank[:] for bank in first_banks], [bank[:] for bank in second_banks]]
        for h in halves:
            for j in range(PACK):
                first_product(right_states[h][j], 1, j, cols[h])

        def quantize_q(e):
            nc.vector.quantize_mx(out=q_codes[:, e, :].bitcast(FP8X4), scales=q_scales[e][:], in_=q_bf[e][:].rearrange("p r j -> p (r j)"))

        for h in halves:
            for j in range(PACK):
                nc.vector.scalar_tensor_tensor(
                    fa_flat[h][:, j, :], right_states[h][j], area_size[:, j : j + 1], left_pairs[j // 2][:, j % 2, cols[h]], ALU.mult, ALU.min
                )
        interleave(nc.scalar.copy, fa_bf[0][:], fa_flat[0][:], 4)
        quantize_q(1)

        def quantize_fa(h):
            nc.vector.quantize_mx(out=fa_codes[h][:].bitcast(FP8X4), scales=fa_scales[h][:], in_=fa_bf[h][:].rearrange("p m j -> p (m j)"))

        quantize_fa(0)
        interleave(nc.vector.tensor_copy, fa_bf[1][:, :VECTOR_COLS, :], fa_flat[1][:, :, :VECTOR_COLS], 4)
        interleave(nc.scalar.copy, fa_bf[1][:, VECTOR_COLS:, :], fa_flat[1][:, :, VECTOR_COLS:], 4)
        quantize_q(0)
        quantize_fa(1)

        def second_product(bank, e, h):
            nc.tensor.matmul_mx(
                out=bank,
                lhsT=q_codes[:, e, :].bitcast(FP8X4),
                lhsT_scale=q_scales[e][:],
                rhs=fa_codes[h][:].bitcast(FP8X4),
                rhs_scale=fa_scales[h][:],
                start=True,
                stop=True,
            )

        out_view = out.rearrange("(e p) m -> p e m", p=P)
        for h in halves:
            for e in reversed(range(R // P)):
                acc = ps.tile([P, HALF], F32, name=f"acc{h}{e}", tag=f"bank{PACK + 2 * h + e}")
                second_product(acc[:], e, h)
                nc.vector.scalar_tensor_tensor(result[h][:, e, :], acc[:], -0.5, cur_sb[:, e, cols[h]], ALU.mult, ALU.add)
                (nc.scalar, nc.sync)[e].dma_start(out_view[:, e, cols[h]], result[h][:, e, :])
